import numpy as np, ml_dtypes
CORES = [40,41,42,43,44,45,46,47]
N = 8
BF = ml_dtypes.bfloat16
V, L, A, T = 4096, 192, 1024, 4
H = L // 2; B = V - T * H
def draw0(rng):
    ax = np.clip(np.floor(rng.random((N, 8, 1, V)) * 300 - 22 + 140 * (rng.random((N, 8, 16, V)) - 0.5)), 0, 255).astype(np.int64)
    zp = np.clip(np.floor(rng.random((N, 8, 1, A)) * 170 + 40 + 160 * (rng.random((N, 8, 16, A)) - 0.5)), 0, 255).astype(np.int64)
    p = np.clip(np.floor(rng.random((N, 8, 1, L)) * 130 + 60 + 160 * (rng.random((N, 8, 16, L)) - 0.5)), 0, 255).astype(np.int64)
    near = (rng.random((N, 8, 1, H)) < 0.6) & (rng.random((N, 8, 16, H)) > 0.15)
    p[..., 1::2] = np.where(near, p[..., ::2], p[..., 1::2])
    rt = rng.integers(0, V, (N, 8, 16, A)); ex = rng.integers(0, V, (N, 8, 16, L))
    ex[..., 1::2] = np.where(rng.random((N, 8, 16, H)) < 0.2, ex[:, :, ::-1, ::2], ex[..., 1::2])
    return ax, rt, zp, ex, p, rng.integers(0, 4096, (N, 8, 16)), rng.integers(0, 4096, (N, 8, 16))
def pack(ax, rt, zp, ex, p, wt, km):
    b = lambda a: np.ascontiguousarray(a.reshape(N, 128, -1)).astype(np.float32).astype(BF)
    w = lambda a: np.ascontiguousarray(a.reshape(N, 128, -1)).astype(np.int32)
    return {"ax": b(ax), "rt": w(rt), "zp": b(zp), "ex": w(ex), "p0": b(p), "wt": w(wt), "km": w(km)}
def setup_inputs(rng):
    return pack(*draw0(rng))
def setup_inputs_spread(rng):
    def uneven(n): return np.minimum(np.floor(np.exp2(1 + 7.3 * rng.random((N, 8, 1, n))) * rng.random((N, 8, 16, n))), 255).astype(np.int64)
    ax, zp, p = uneven(V), uneven(A), uneven(L)
    p[..., 1::2] = np.where(rng.random((N, 8, 1, H)) < 0.4, p[..., ::2], p[..., 1::2])
    rt = np.minimum(np.floor(V * rng.random((N, 8, 16, A)) ** (0.5 + 3 * rng.random((N, 8, 1, A)))), V - 1).astype(np.int64)
    ex = np.minimum(np.floor(V * rng.random((N, 8, 16, L)) ** (0.5 + 3 * rng.random((N, 8, 1, L)))), V - 1).astype(np.int64)
    wt = np.minimum(np.floor(np.exp2(12.1 * rng.random((N, 8, 16)))) - 1, 4095).astype(np.int64)
    km = np.minimum(np.floor(np.exp2(12.1 * rng.random((N, 8, 16)))) - 1, 4095).astype(np.int64)
    return pack(ax, rt, zp, ex, p, wt, km)
def setup_inputs_ends(rng):
    den = np.array([0.0, 0.1, 0.25, 0.5, 0.75, 1.0])
    ax = 255 * (rng.random((N, 8, 16, V)) < rng.choice(den, (N, 8, 1, V))); zp = 255 * (rng.random((N, 8, 16, A)) < rng.choice(den, (N, 8, 1, A)))
    p = 255 * (rng.random((N, 8, 16, L)) < rng.choice(np.array([0.0, 0.25, 0.5, 0.75, 0.9, 1.0]), (N, 8, 1, L)))
    p[..., 1::2] = np.where(rng.random((N, 8, 1, H)) < 0.5, p[..., ::2], p[..., 1::2])
    for g, (a, b) in enumerate(((0.0, 0.4), (0.2, 1.0), (0.3, 0.7), (0.4, 0.0), (0.5, 0.3), (0.7, 0.2), (1.0, 0.3), (0.3, 0.5))):
        ax[:, g, :, 0] = 255 * (rng.random((N, 16)) < a); ax[:, g, :, V - 1] = 255 * (rng.random((N, 16)) < b)
    def names(n): return np.where(rng.random((N, 8, 16, n)) < 0.85, (V - 1) * rng.integers(0, 2, (N, 8, 16, n)), rng.integers(0, V, (N, 8, 16, n)))
    rt, ex = names(A), names(L)
    wt = 4095 * rng.integers(0, 2, (N, 8, 16)); km = 4095 * rng.integers(0, 2, (N, 8, 16))
    wt[:, 7] = 4095; wt[:, 5:7, 15] = 4095; wt[:, 0, 0] = 0; wt[:, 0, 1] = 4095
    for m, k in ((0, 0), (1, 4095), (3, 8), (9, 3856), (15, 3841)): km[:, 5:, m] = k
    one = np.zeros(16, np.int64); one[15] = 1
    for i in (0, 1, L - 2, L - 1): p[:, 5:, :, i] = one
    for i in (2, 3, L - 4, L - 3): p[:, 7, :, i] = 255; p[:, 6, :, i] = 0
    p[N - 1, 7, :, L - 2:] = 255
    for h in (3840, 3841, 4095, 4080, 3832): zp[:, 5:, :, (h * A) >> 12] = 255
    zp[:, 6, :, (4080 * A) >> 12] = 0; zp[:, 6, :, (4095 * A) >> 12] = 0; zp[:, 5, :, (4095 * A) >> 12] = 0
    for h in (8, 4088, 24, 264, 136): zp[:, 7, :, (h * A) >> 12] = 0
    zp[:, 6, :, 0] = 255
    return pack(ax, rt, zp, ex, p, wt, km)
def setup_inputs_corners(rng):
    ax, rt, zp, ex, p, wt, km = draw0(rng)
    cnt = rng.integers(0, 17, (N, 8, 1, V)); cnt[..., :17] = np.arange(17)
    hi = ((np.arange(16)[:, None] + rng.integers(0, 16, (N, 8, 1, V))) & 15) < cnt
    ax = np.where(hi, rng.integers(139, 256, ax.shape), rng.integers(0, 111, ax.shape))
    p = rng.integers(111, 140, p.shape); p[..., 1::2] = np.where(rng.random((N, 8, 1, H)) < 0.5, p[..., ::2], p[..., 1::2])
    sets = ((0, 1, 2, 3), (9, 10, 12, 16), (3, 4), (4, 5, 6, 7, 8), (8, 9), tuple(range(17)), (8,), ())
    full = int(rng.integers(0, N))
    for q in range(N):
        for g in range(8):
            s = 0 if q == full else (q + g) & 7
            cand = np.flatnonzero(np.isin(cnt[q, g, 0], np.array(sets[s], np.int64))) if s < 7 else np.array([0, B - 1, B, B + H - 1, B + H, V - 2, V - 1])
            if s == 6: cand = cand[:1]
            rt[q, g] = cand[rng.integers(0, len(cand), (16, A))]
    nm = (rng.integers(0, V, (N, 8, 1, H)) + (2 * rng.integers(0, V // 2, (N, 8, 1, H)) + 1) * np.arange(32)[:, None]) & (V - 1)
    ea, eb = nm[:, :, :16], nm[:, :, 16:]; rep = np.broadcast_to(nm[:, :, :1], ea.shape)
    kd = (np.arange(H)[None, None, None, :] + np.arange(8)[None, :, None, None] + np.arange(N)[:, None, None, None]) % 6
    lone = eb.copy(); lone[:, :, 0] = ea[:, :, 15]
    ex[..., ::2] = np.where(kd >= 4, rep, ea)
    ex[..., 1::2] = np.where(kd == 0, ea, np.where(kd == 1, ea[:, :, ::-1], np.where(kd == 3, lone, np.where(kd == 4, rep, eb))))
    ch = rng.integers(0, 3, (N, 8, 1, A)); ch[:, 1] = 0
    zp = np.take_along_axis(rng.integers(0, 256, (N, 8, 16, 3)), ch, 3)
    km[:, 2] = rng.integers(0, 4096, (N, 1)); km[:, 3, ::2] = 0; km[:, 3, 1::2] = 4095; wt[:, 4] = 0; wt[:, 6, 1:] = 0; wt[:, 6, 0] = 4095
    return pack(ax, rt, zp, ex, p, wt, km)
def setup_inputs_alike(rng):
    ax, rt, zp, ex, p, wt, km = draw0(rng)
    p[:, ::2] = p[:, ::2, :, :1]
    p[:, 1::2] = np.take_along_axis(p[:, 1::2, :, :4], rng.integers(0, 4, (N, 4, 1, L)), 3)
    rt = np.take_along_axis(rt[..., :8], rng.integers(0, 8, (N, 8, 1, A)), 3)
    rt[:, 3] = rng.choice(np.array([0, V - 1, B, B - 1]), (N, 16, A))
    ex[:, ::2] = rng.choice(np.array([0, 5, B - 1, B, B + H, V - 1]), (N, 4, 16, L))
    zp[:, 4:] = np.take_along_axis(zp[:, 4:, :, :16], rng.integers(0, 16, (N, 4, 1, A)), 3)
    wt[:, 5, :14] = rng.integers(3200, 4096, (N, 14)); wt[:, 5, 14] = 256; wt[:, 5, 15] = 1
    aim = np.array([0, 4095, 4075, 4077, 4087])[np.arange(H // 2) % 5]
    big = rng.integers(200, 256, (N, 14, H // 2))
    rest = (4096 + aim - np.sum(wt[:, 5, :14, None] * big, axis=1)) & 8191
    p[:, 5, :14, 2::4] = big; p[:, 5, 14, 2::4] = rest >> 8; p[:, 5, 15, 2::4] = rest & 255; p[:, 5, :, 3::4] = 0
    for k, v in ((5, V - 3), (6, V - 5), (7, V - 7)):
        rt[:, 5, k] = v; ax[:, 5, :, v] = 0; ax[:, 5, :4, v] = 255; ax[:, 5, 14:, v] = 255
    for v, u in ((V - 3, 4075), (V - 5, 4077), (V - 7, 4087), (V - 3, 4095), (V - 3, 4096)): ax[:, 5, :, (((v * u) >> 5) + v) & (V - 1)] = 255
    return pack(ax, rt, zp, ex, p, wt, km)
def check_inputs(d):
    bad = []
    for k, hi in (("ax", 255), ("rt", V - 1), ("zp", 255), ("ex", V - 1), ("p0", 255), ("wt", 4095), ("km", 4095)):
        v = np.asarray(d[k]).astype(np.float64)
        if not (np.min(v) >= 0 and np.max(v) <= hi): bad.append("range of " + k)
        elif np.any(v != np.floor(v)): bad.append("whole numbers of " + k)
    return bad
def pick(x, e):
    n = e.shape[3]
    return np.take_along_axis(x, e.reshape(N, 8, 1, 16 * n), 3).reshape(N, 8, 16, 16, n)
def reference(ax, rt, zp, ex, p0, wt, km):
    x = ax.astype(np.float32).astype(np.int64).reshape(N, 8, 16, V)
    r = np.zeros((N, 8, 16, A + T * L), np.int64); z = np.zeros((N, 8, 16, A + T * L), np.int64)
    r[..., :A] = rt.reshape(N, 8, 16, A); z[..., :A] = zp.astype(np.float32).astype(np.int64).reshape(N, 8, 16, A)
    e0 = ex.astype(np.int64).reshape(N, 8, 16, L); p = p0.astype(np.float32).astype(np.int64).reshape(N, 8, 16, L)
    w = wt.astype(np.int64).reshape(N, 8, 16, 1); k = km.astype(np.int64).reshape(N, 8, 16, 1); odd = np.zeros(N, np.int64)
    for t in range(T):
        n = A + L * t
        u = np.repeat(np.add.reduce(w * p, axis=2)[:, :, ::2] & 4095, 2, axis=2)[:, :, None, :]
        c = (((((u * u) >> 5) & 4095) + ((k * u) & 4095)) & 4095) * n >> 12
        score = np.sum(np.abs(pick(z, c) - p[:, :, :, None, :]), axis=2)
        a = np.minimum.reduce(score * 4096 + c, axis=2) & 4095
        e = np.take_along_axis(r, a[:, :, None, :], 3)
        v = np.sum(pick(x, e) >= p[:, :, :, None, :], axis=2)
        barred = v < 4 + odd[:, None, None, None]
        e2 = (((e * u) >> 5) + e + 77 * t) & (V - 1)
        v2 = np.sum(pick(x, e2) >= p[:, :, :, None, :], axis=2)
        f = np.where(barred, e0, np.where((v < 9) & (v2 >= v), e2, e))
        odd = np.sum(barred, axis=(1, 2, 3)) & 1
        fa, fb = f[..., ::2].copy(), f[..., 1::2].copy()
        same = fa[:, :, :, None, :] == fb[:, :, None, :, :]
        ca, cb = np.any(same, axis=3), np.any(same, axis=2)
        rec = np.maximum.reduce(np.where(ca[:, :, None], pick(x, fa), 0), axis=3)
        new = B + H * t + np.arange(H)
        f[..., ::2] = np.where(ca, new, fa); f[..., 1::2] = np.where(cb, new, fb)
        src = (np.arange(N) - 1 - t % 3) % N
        f, p = f[src], p[src]
        r[..., n:n + L] = f
        if t < T - 1: z[..., n:n + L] = p
        x[..., B + H * t:B + H * t + H] = rec[src]
        p = (p + 255 - np.take_along_axis(x, f[:, :, :1], 3)) >> 1
    return {"yr": r[..., A:].reshape(N, 128, T * L).astype(np.float32), "yp": p.reshape(N, 128, L).astype(np.float32)}

from concourse.mybir import dt, AluOpType as A, ActivationFunctionType as F

V, L, A0, TT = 4096, 192, 1024, 4
H = L // 2
XW = V + 512
RW = A0 + TT * L
CFG = {
    "CH": ((0, 48), (48, 96)),
    "ZP": ("SVS", "SSV"),
    "VP": (("VVS", "VVS"), ("VVS", "SSV")),
    "RG": ("S", "B"),
    "PS": (6, 4),
    "ORD": "h0 p0 h1 p1 s z0 E0 z1 E1 v00 v01 c0 v10 m0 v11 c1 m1",
    "SLACK": 15.0, "SPL": 1, "PR": {},
}
DT = {"i": "int32", "u": "uint16", "f": "float32", "b": "bfloat16", "h": "float16"}
ARENA = {"i": 4096, "u": 1024, "f": 2560, "b": 24576, "h": 5120}
SCRATCH = {
    "X": ("sbuf", [128, XW], "bfloat16"), "Xh": ("sbuf", [128, V], "bfloat16"), "Z": ("sbuf", [128, RW], "bfloat16"),
    "R": ("sbuf", [128, RW], "float32"), "ri": ("sbuf", [128, A0], "int32"), "exi": ("sbuf", [128, L], "int32"),
    "wi": ("sbuf", [128, 1], "int32"), "ki": ("sbuf", [128, 1], "int32"),
    "pn": ("sbuf", [128, TT * L], "bfloat16"), "fnat": ("sbuf", [128, TT * L], "float32"), "yo": ("sbuf", [128, L], "float32"),
    "f0s": ("sbuf", [128, TT * 16], "uint16"), "f0l": ("sbuf", [128, TT * 16], "uint16"),
    "qs": ("sbuf", [128, TT * H], "bfloat16"), "ql": ("sbuf", [128, TT * H], "bfloat16"),
}
for _k in ARENA:
    SCRATCH["ar_" + _k] = ("sbuf", [128, ARENA[_k]], DT[_k])
PS = ("d0", "d1", "d2", "d3", "v1", "v2", "sc", "cm")
for _n in PS:
    SCRATCH[_n] = ("psum", [128, 512], "float32")
LOADS = ("p0", "wt", "km", "zp", "rt", "ax", "ex")
SEMAPHORES = ["cV", "cS", "cP", "cG", "sent", "stored"] + ["ld_" + n for n in LOADS] + ["ar_%s%d" % (k, t) for t in range(TT) for k in "pfqz"]
RATE = {"V": 1.0, "S": 1.0, "P": 0.5, "G": 1.0}
EST = {"gather": 1.56, "wake": 90.0, "dma": 2200.0, "send": 2300.0}
WHERE = {}
TOP = {}


def need(kind, **names):
    q = {"i": 8, "f": 8, "b": 16, "u": 16, "h": 16}[kind]
    for n, w in names.items():
        WHERE[n] = (kind, TOP.get(kind, 0))
        TOP[kind] = TOP.get(kind, 0) + -(-w // q) * q


def ap(T, n, lo, hi, st=1):
    if n in WHERE:
        k, o = WHERE[n]
        n, lo, hi = "ar_" + k, lo + o, hi + o
    return T[n][:, lo:hi:st] if st > 1 else T[n][:, lo:hi]


def is32(n):
    return WHERE[n][0] == "f" if n in WHERE else SCRATCH[n][2] == "float32"


def rg_(b, lo, hi, st=1):
    return (b, lo, hi, st, lo % st)


def build():
    WHERE.clear()
    TOP.clear()
    CH = CFG["CH"]
    GC = EST["gather"]
    NC = range(len(CH))
    ops = []

    def op(eng, cyc, w, r, fn, kind="c", name="", fix=0.0):
        w, r = [x if len(x) == 5 else rg_(*x) for x in w], [x if len(x) == 5 else rg_(*x) for x in r]
        ops.append({"e": eng, "c": cyc * 0.83 * RATE.get(eng, 1.0) + fix, "w": w, "r": r, "f": fn, "k": kind, "n": name})

    def v(n, w, r, fn, name="", half=False, fix=0.0):
        op("V", max(64, n * (0.5 if half else 1)), w, r, fn, name=name, fix=fix)

    def s(n, w, r, fn, name="", fix=0.0):
        op("S", max(64, n), w, r, fn, name=name, fix=fix)

    def vm(buf, lo, hi, val, st=1):
        v(hi - lo, [(buf, lo, hi)], [], lambda T, g: g.vector.memset(ap(T, buf, lo, hi, st), val), "memset", half=True)

    def gsel(out, inp, n, pat, cmp_, base, cm, at=0):
        op("G", 2 * n, [(out, at, at + n)], [(inp, 0, n)], lambda T, g: g.affine_select(ap(T, out, at, at + n), ap(T, inp, 0, n), pat, cmp_, 0.0, base, cm), fix=170, name="sel")

    def giota(out, n, pat, base, cm, fl=True):
        op("G", 2 * n, [(out, 0, n)], [], (lambda T, g: g.iota(ap(T, out, 0, n), pat, base, cm, allow_small_or_imprecise_dtypes=True)) if fl else (lambda T, g: g.iota(ap(T, out, 0, n), pat, base, cm)), fix=130, name="iota")

    def vs(out, ol, oh, inp, il, ih, s1, op0, s2=None, op1=None, half=False, ost=1, ist=1, name="", scol=None):
        def fn(T, g):
            sc = ap(T, scol[0], scol[1], scol[1] + 1) if scol else s1
            o, i = ap(T, out, ol, oh, ost), ap(T, inp, il, ih, ist)
            if op1 is None:
                return g.vector.tensor_scalar(o, i, sc, None, op0)
            return g.vector.tensor_scalar(o, i, sc, s2, op0, op1)
        v(-(-(ih - il) // ist), [(out, ol, oh, ost)], [(inp, il, ih, ist)] + ([(scol[0], scol[1], scol[1] + 1)] if scol else []), fn, name, half)

    def vc(out, ol, oh, inp, il, ih, half=False, ost=1, ist=1, name=""):
        v(-(-(ih - il) // ist), [(out, ol, oh, ost)], [(inp, il, ih, ist)], lambda T, g: g.vector.tensor_copy(ap(T, out, ol, oh, ost), ap(T, inp, il, ih, ist)), name, half)

    def vt(out, ol, oh, a, al, ah, b, bl, bh, o_, name=""):
        n = ah - al
        v(n if (a in PS or b in PS) else 2 * n, [(out, ol, oh)], [(a, al, ah), (b, bl, bh)],
          lambda T, g: g.vector.tensor_tensor(ap(T, out, ol, oh), ap(T, a, al, ah), ap(T, b, bl, bh), o_), name)

    def act(out, ol, oh, inp, il, ih, fn_, ost=1, ist=1, bias=0.0, scale=1.0, bcol=None, acc=None, name=""):
        def fn(T, g):
            kw = {"scale": scale, "bias": ap(T, bcol, 0, 1) if bcol else bias}
            if acc:
                kw["accum_out"] = ap(T, acc[0], acc[1], acc[1] + 1)
            return g.scalar.activation(ap(T, out, ol, oh, ost), ap(T, inp, il, ih, ist), fn_, **kw)
        s(-(-(ih - il) // ist), [(out, ol, oh, ost)] + ([(acc[0], acc[1], acc[1] + 1)] if acc else []), [(inp, il, ih, ist)] + ([(bcol, 0, 1)] if bcol else []), fn, name)

    def gather_v(out, ol, oh, win, wh, off, fl, fh, name, in1=None, o_=None):
        def fn(T, g):
            ind = T[win][:, 0:wh].indirect(ap(T, off, fl, fh))
            if in1 is None:
                return g.vector.tensor_copy(ap(T, out, ol, oh), ind)
            return g.vector.tensor_tensor(ap(T, out, ol, oh), ind, ap(T, *in1), o_)
        v((oh - ol) * GC, [(out, ol, oh)], [(win, 0, wh), (off, fl, fh)] + ([in1] if in1 else []), fn, name, fix=50)

    def gather_s(out, ol, oh, win, wh, off, fl, fh, name):
        s((oh - ol) * GC, [(out, ol, oh)], [(win, 0, wh), (off, fl, fh)],
          lambda T, g: g.scalar.activation(ap(T, out, ol, oh), T[win][:, 0:wh].indirect(ap(T, off, fl, fh)), F.Copy), name, fix=65)

    def groups(grs, name):
        cost, w, r = 0, [], []
        for prs, out, ol, oh, ost in grs:
            w.append((out, ol, oh, ost))
            for x in prs:
                n = -(-(x[5] - x[4]) // x[6])
                cost += max(min(64, x[2] - x[1]), n) * (4 if is32(x[3]) else 1)
                r += [(x[0], x[1], x[2], 1), x[3:7]]

        def fn(T, g):
            ins = None
            for prs, out, ol, oh, ost in grs:
                for y, x in enumerate(prs):
                    ins = g.tensor.matmul(ap(T, out, ol, oh, ost), ap(T, x[0], x[1], x[2]), ap(T, x[3], x[4], x[5], x[6]), y == 0, y == len(prs) - 1)
            return ins
        op("P", cost, w, sorted(set(r)), fn, name=name)

    bank = [0]

    def dbank():
        bank[0] = (bank[0] + 1) % 4
        return "d%d" % bank[0]

    need("b", ones=144, tmpa=144, tmpb=144, BB=128, W8=144, W4=144, I1=128, IN=128, I8=128, IB=128, IC=128, BG=128, smax=1536, p=L, prep=L * 16)
    need("f", ones32=128, cf=8, id32=128, up32=128, dn32=128, iot=16, iom=L, ion=H, M16=16, smin=L, pc=L, bar=1, cb=8)
    need("h", WH=128, WL=128, J1=128, JN=128, BS=2048, Q=512, N16=TT * H, E16=L, p16=L, mk=H)
    need("i", ci=8, cj=8)
    for c in NC:
        np_ = CH[c][1] - CH[c][0]
        nl, C = 2 * np_, str(c)
        need("i", **{x + C: w for x, w in (("si", np_), ("ul", nl), ("uu", np_), ("uv", np_), ("ku", np_), ("li", 12), ("t1", nl), ("t3", nl), ("fe", nl), ("f", nl), ("ff", nl))})
        need("u", **{x + C: w for x, w in (("cl", np_), ("al", 12), ("el", nl), ("e2l", nl), ("lu", np_))})
        need("f", **{x + C: w for x, w in (("kt", nl), ("ks", nl), ("ef", nl), ("k1", nl), ("rl", np_))})
        need("h", **{x + C: w for x, w in (("c16", nl), ("lh", 12), ("f16", nl), ("F16", nl), ("FT", nl))})
        need("b", **{x + C: w for x, w in (("gz", 16 * np_), ("dz", 16 * nl), ("g1", 16 * nl), ("g2", 16 * nl), ("x1", 16 * nl), ("bb", nl), ("eq", 16 * np_), ("rs", 16 * np_))})

    for q, nm, buf, wid in (("Y", "p0", "pn", L), ("Y", "wt", "wi", 1), ("Y", "km", "ki", 1), ("SD", "zp", "Z", A0), ("Y", "ax", "X", V), ("SD", "rt", "ri", A0), ("Y", "ex", "exi", L)):
        op(q, 0, [(buf, 0, wid)], [], (lambda T, q_, nm=nm, buf=buf, wid=wid: q_.dma_start(T[buf][:, 0:wid], T[nm][:, :])), kind="load", name=nm)
    vm("ones", 0, 144, 1.0)
    vm("ones32", 0, 128, 1.0)
    gsel("tmpa", "ones", 128, [[-16, 8], [0, 16]], A.is_ge, 0, 1)
    gsel("BB", "tmpa", 128, [[16, 8], [0, 16]], A.is_ge, 15, -1)
    vs("ci", 0, 1, "wi", 0, 1, 63, A.bitwise_and)
    vc("cf", 0, 1, "ci", 0, 1)
    vt("cf", 1, 2, "wi", 0, 1, "ci", 0, 1, A.subtract)
    vc("cf", 2, 3, "ki", 0, 1)
    vs("WH", 0, 128, "BB", 0, 128, None, A.mult, scol=("cf", 1), half=True)
    vs("WL", 0, 128, "BB", 0, 128, None, A.mult, scol=("cf", 0), half=True)
    vs("mk", 0, H, "ones", 0, H, -1024.0, A.mult, half=True)
    gsel("id32", "ones32", 128, [[-1, 128]], A.is_equal, 0, 1)
    vc("I1", 0, 128, "id32", 0, 128)
    vs("IN", 0, 128, "id32", 0, 128, -1.0, A.mult)
    for c, (j0, j1) in enumerate(CH):
        m = j1 - j0
        for b in (0, 1):
            vs("p16", 2 * j0 + b * m, 2 * j0 + b * m + m, "pn", 2 * j0 + b, 2 * j1, 1024.0, A.add, half=True, ist=2)
        vs("p", 2 * j0, 2 * j1, "p16", 2 * j0, 2 * j1, -1024.0, A.add, half=True, name="p")
    act("cb", 0, 4, "ones32", 0, 4, F.Sigmoid, name="table")

    def setup():
        gsel("tmpb", "ones", 144, [[-16, 9], [-1000, 16]], A.is_ge, 16, 1)
        gsel("tmpa", "tmpb", 144, [[16, 9], [0, 16]], A.is_ge, -1, -1)
        vs("W4", 0, 144, "tmpa", 0, 144, 4096.0, A.mult, half=True)
        vs("J1", 0, 128, "id32", 0, 128, 1.0, A.mult)
        giota("iom", L, [[0, L // 16], [1, 16]], 0, 0)
        vs("smin", 0, L, "iom", 0, L, 0.0, A.is_equal, 33554432.0, A.mult)
        giota("cj", 1, [[1, 1]], 0, 1, fl=False)
        vs("ci", 1, 2, "cj", 0, 1, 4, A.logical_shift_right, 1, A.bitwise_and)
        vc("cf", 4, 5, "ci", 1, 2)
        vs("cf", 5, 6, "ci", 1, 2, -1.0, A.mult, 1.0, A.add)
        gsel("up32", "ones32", 128, [[-1, 128]], A.is_equal, 16, 1)
        gsel("dn32", "ones32", 128, [[-1, 128]], A.is_equal, -16, 1)
        vs("Q", 0, 128, "id32", 0, 128, None, A.mult, scol=("cf", 5))
        vs("Q", 384, 512, "id32", 0, 128, None, A.mult, scol=("cf", 4))
        vs("Q", 128, 256, "up32", 0, 128, None, A.mult, scol=("cf", 5))
        vs("Q", 256, 384, "dn32", 0, 128, None, A.mult, scol=("cf", 4))
        vc("R", 0, A0, "ri", 0, A0, name="R")
        vm("X", V, XW, 0.0)
        vm("bar", 0, 1, -1280.0)
        vs("W8", 0, 144, "tmpa", 0, 144, 8192.0, A.mult, half=True)
        vs("BG", 0, 128, "BB", 0, 128, -4352.0, A.mult, half=True)
        vs("IB", 0, 128, "I1", 0, 128, 1048576.0, A.mult, half=True)
        vs("IC", 0, 128, "I1", 0, 128, -129024.0, A.mult, half=True)
        for c, (j0, j1) in enumerate(CH):
            m = j1 - j0
            for b in (0, 1):
                vs("E16", 2 * j0 + b * m, 2 * j0 + b * m + m, "exi", 2 * j0 + b, 2 * j1, -2048.0, A.add, ist=2)
        vs("I8", 0, 128, "I1", 0, 128, 8192.0, A.mult, half=True)
        vs("JN", 0, 128, "id32", 0, 128, -1.0, A.mult)
        vs("ci", 2, 3, "cj", 0, 1, 15, A.bitwise_and)
        vc("cf", 3, 4, "ci", 2, 3)
        giota("iot", 16, [[1, 16]], 0, 0)
        vs("M16", 0, 16, "iot", 0, 16, None, A.is_equal, scol=("cf", 3))
        for k in range(16):
            vs("BS", 128 * k, 128 * k + 128, "BB", 0, 128, None, A.mult, scol=("M16", k), half=True)
        giota("ion", H, [[1, H]], -384, 0)
        for t in range(TT):
            vs("N16", H * t, H * t + H, "ion", 0, H, float(H * t), A.add)
        vm("smax", 0, 1536, 1.0)
        vm("smax", 0, 1536, 0.0, st=16)
        for k in range(4):
            vs("Xh", 1024 * k, 1024 * k + 1024, "X", 1024 * k, 1024 * k + 1024, -0.5, A.mult, half=True, name="Xh")

    def hash_(t, c):
        n, (j0, j1), C = A0 + L * t, CH[c], str(c)
        a, m, o = 2 * j0, j1 - j0, 416 + j0
        groups([([(x, 0, 128, "mk", 0, m, 1) for x in ("WH", "WL")] + [(x, 0, 128, "p16", a, a + m, 1) for x in ("WH", "WL")], "sc", o, o + m, 1)], "u")
        vc("si" + C, 0, m, "sc", o, o + m, name="si")
        vs("ul" + C, 0, m, "si" + C, 0, m, 4095, A.bitwise_and, name="u")
        vt("uu" + C, 0, m, "ul" + C, 0, m, "ul" + C, 0, m, A.mult, "uu")
        vs("ku" + C, 0, m, "ul" + C, 0, m, None, A.mult, scol=("cf", 2), name="ku")
        vs("uv" + C, 0, m, "uu" + C, 0, m, 5, A.arith_shift_right, 4095, A.bitwise_and, name="uv")
        vt("uu" + C, 0, m, "ku" + C, 0, m, "uv" + C, 0, m, A.add, "hh")
        vs("si" + C, 0, m, "uu" + C, 0, m, 4095, A.bitwise_and, name="hm")
        vs("cl" + C, 0, m, "si" + C, 0, m, n / 4096.0, A.mult, -0.5 + 2.0 ** -13, A.add, name="cl")
        for b in (0, 1):
            vc("c16" + C, b * m, b * m + m, "cl" + C, 0, m, half=True, name="c16")
        vc("ul" + C, m, 2 * m, "ul" + C, 0, m, name="uB")

    def prep(c):
        j0, j1 = CH[c]
        for k in range(16):
            if k < CFG["PS"][c]:
                act("prep", 32 * j0 + k, 32 * j1, "p", 2 * j0, 2 * j1, F.Copy, ost=16, name="prep")
            else:
                vc("prep", 32 * j0 + k, 32 * j1, "p", 2 * j0, 2 * j1, half=True, ost=16, name="prep")

    def zstage(t, c):
        n, (j0, j1), C = A0 + L * t, CH[c], str(c)
        b, m, path = 2 * j0, j1 - j0, CFG["ZP"][c]
        for x, pa in enumerate(path):
            j = 16 * x
            if pa == "S":
                gather_s("gz" + C, 16 * j, 16 * j + 256, "Z", n, "cl" + C, j, j + 16, "Zg")
                d = dbank()
                groups([([("I1", 0, 128, "gz" + C, 16 * j, 16 * j + 256, 1), ("IN", 0, 128, "prep", 16 * (b + h * m + j), 16 * (b + h * m + j) + 256, 1)], d, 256 * h, 256 * h + 256, 1) for h in (0, 1)], "Zsub")
            for h in (0, 1):
                l = 16 * (h * m + j)
                if pa == "S":
                    act("dz" + C, l, l + 256, d, 256 * h, 256 * h + 256, F.Abs, name="Zabs")
                else:
                    gather_v("g1" + C, l, l + 256, "Z", n, "cl" + C, j, j + 16, "Zfused", in1=("prep", 16 * b + l, 16 * b + l + 256), o_=A.subtract)
                    act("dz" + C, l, l + 256, "g1" + C, l, l + 256, F.Abs, name="Zabs")

    def relay(src, so, st, out, o0, q):
        return [([("Q", 256 * hi + 128 * gl, 256 * hi + 128 * gl + 128, src, so + st * gl, st * q, 2 * st) for gl in (0, 1)], out, o0 + hi, o0 + q, 2) for hi in (0, 1)]

    def elect(t, c):
        n, (j0, j1), C = A0 + L * t, CH[c], str(c)
        m, o = j1 - j0, 2 * j0
        nl = 2 * m
        q = nl // 16
        r0 = 208 + 16 * c
        groups([([("W4", 16 - k, 144 - k, "dz" + C, k, nl * 16, 16) for k in range(16)] + [("J1", 0, 128, "c16" + C, 0, nl, 1)], "sc", o, o + nl, 1)], "score")
        v(nl, [("kt" + C, 0, nl)], [("sc", o, o + nl)], lambda T, g: g.vector.transpose(ap(T, "kt" + C, 0, nl), ap(T, "sc", o, o + nl)), "kT")
        v(nl, [("ks" + C, 0, nl)], [("kt" + C, 0, nl), ("smin", 0, nl)],
          lambda T, g: g.vector.tensor_tensor_scan(ap(T, "ks" + C, 0, nl), ap(T, "smin", 0, nl), ap(T, "kt" + C, 0, nl), 33554432.0, A.max, A.min), "kmin")
        vc("li" + C, 0, q, "ks" + C, 15, nl, ist=16, name="li")
        vs("li" + C, 0, q, "li" + C, 0, q, 4095, A.bitwise_and, name="lm")
        vc("lh" + C, 0, q, "li" + C, 0, q, name="lh")
        groups(relay("lh" + C, 0, 1, "sc", r0, q), "relay")
        vc("al" + C, 0, q, "sc", r0, r0 + q, name="al")
        gather_v("el" + C, 0, nl, "R", n, "al" + C, 0, q, "eL")
        gather_v("t1" + C, 0, nl, "R", n, "al" + C, 0, q, "eu", in1=("ul" + C, 0, nl), o_=A.mult)
        gather_s("ef" + C, 0, nl, "R", n, "al" + C, 0, q, "ef")
        e7 = "ef" + C
        if t:
            e7 = "kt" + C
            act(e7, 0, nl, "ef" + C, 0, nl, F.Identity, bias=float(77 * t), name="e77")
        vs("t1" + C, 0, nl, "t1" + C, 0, nl, 5, A.arith_shift_right, name="t2")
        vt("t3" + C, 0, nl, "t1" + C, 0, nl, e7, 0, nl, A.add, "t3")
        vs("t3" + C, 0, nl, "t3" + C, 0, nl, 4095, A.bitwise_and, name="e2")
        vc("e2l" + C, 0, nl, "t3" + C, 0, nl, name="e2L")

    def vstage(t, c, w):
        (j0, j1), C = CH[c], str(c)
        b, lst, gb = 2 * j0, ("el", "e2l")[w] + C, ("g1", "g2")[w] + C
        path = CFG["VP"][c][w]
        x = 0
        while x < len(path):
            if path[x] == "V":
                y = x
                while y < len(path) and path[y] == "V" and (y == x or not CFG["SPL"]):
                    y += 1
                gather_v(gb, 512 * x, 512 * y, "X", XW, lst, 32 * x, 32 * y, "votes", in1=("prep", 16 * b + 512 * x, 16 * b + 512 * y), o_=A.is_ge)
                x = y
            else:
                gather_s("x1" + C, 512 * x, 512 * x + 512, "X", XW, lst, 32 * x, 32 * x + 32, "votesS")
                d = dbank()
                groups([([("I1", 0, 128, "x1" + C, 512 * x, 512 * x + 512, 1), ("IN", 0, 128, "prep", 16 * b + 512 * x, 16 * b + 512 * x + 512, 1)], d, 0, 512, 1)], "vsub")
                act(gb, 512 * x, 512 * x + 512, d, 0, 512, F.Sigmoid, bias=128.0, scale=256.0, name="vsig")
                x += 1

    def choice(t, c):
        (j0, j1), C = CH[c], str(c)
        b = 2 * j0
        nl = 2 * (j1 - j0)
        o, o2 = b, 192 + b
        groups([([("BG", 0, 128, "ones", 0, nl, 1)] + [("W8", 16 - k, 144 - k, "g1" + C, k, nl * 16, 16) for k in range(16)], "v1", o, o + nl, 1)], "v1sum")
        act("bb" + C, 0, nl, "v1", o, o + nl, F.Sigmoid, scale=-1.0 / 32, bcol="bar", acc=("cb", c), name="barred")
        vt("k1" + C, 0, nl, "v1", o, o + nl, "ef" + C, 0, nl, A.add, "k1")
        groups([([("J1", 0, 128, "E16", b, b + nl, 1), ("IC", 0, 128, "ones", 0, nl, 1), ("IB", 0, 128, "bb" + C, 0, nl, 1)], "v1", o2, o2 + nl, 1)], "k3")
        groups([([("W8", 16 - k, 144 - k, "g2" + C, k, nl * 16, 16) for k in range(16)], "v2", o, o + nl, 1)], "v2sum")
        act("v2", o2, o2 + nl, "v2", o, o + nl, F.Relu, bias=65536.0, scale=-1.0, name="r")
        vt("v2", o2, o2 + nl, "t3" + C, 0, nl, "v2", o2, o2 + nl, A.subtract, "k2")
        vt("k1" + C, 0, nl, "v2", o2, o2 + nl, "k1" + C, 0, nl, A.max, "max")
        vt("fe" + C, 0, nl, "v1", o2, o2 + nl, "k1" + C, 0, nl, A.max, "max")
        vs("f" + C, 0, nl, "fe" + C, 0, nl, 4095, A.bitwise_and, name="f")
        vs("f16" + C, 0, nl, "f" + C, 0, nl, -2048.0, A.add, name="f16")

    def parity():
        groups([([("ones32", 0, 128, "cb", c, c + 1, 1) for c in NC], "cm", 500, 501, 1)], "par")
        vc("ci", 4, 5, "cm", 500, 501)
        vs("ci", 5, 6, "ci", 4, 5, 1, A.bitwise_and)
        vs("bar", 0, 1, "ci", 5, 6, 256.0, A.mult, -1280.0, A.add)

    def common(t, c):
        (j0, j1), C = CH[c], str(c)
        m = j1 - j0
        nl = 2 * m
        per = 16 if m <= 32 else 8
        for h in range(16 // per):
            d = dbank()
            groups([([("BS", 128 * k, 128 * k + 128, "f16" + C, m, nl, 1), ("JN", 0, 128, "f16" + C, 0, m, 1)], d, m * (k - per * h), m * (k - per * h) + m, 1) for k in range(per * h, per * h + per)], "bcast")
            vs("eq" + C, m * per * h, m * per * h + m * per, d, 0, m * per, 0.0, A.is_equal, name="eq")
        nn = ("J1", 0, 128, "N16", H * t + j0, H * t + j1, 1)
        groups([([nn] + [("I8", 0, 128, "eq" + C, m * k, m * k + m, 1) for k in range(16)], "cm", j0, j1, 1)], "ca")
        act("rl" + C, 0, m, "cm", j0, j1, F.Relu, scale=-1.0, bias=4096.0, name="rl")
        vt("rl" + C, 0, m, "f" + C, 0, m, "rl" + C, 0, m, A.max, "ls")
        vc("lu" + C, 0, m, "rl" + C, 0, m, name="lu")
        b0 = 256 + j0
        groups([([nn] + [("W8", 16 - k, 144 - k, "eq" + C, m * k, m * k + m, 1) for k in range(16)], "sc", b0, b0 + m, 1)], "cb")
        way = CFG["RG"][c]
        if way == "B":
            gather_s("gz" + C, 0, m * 8, "X", XW, "lu" + C, 0, m // 2, "rg")
            gather_v("gz" + C, m * 8, m * 16, "X", XW, "lu" + C, m // 2, m, "rg")
        elif way == "S":
            gather_s("gz" + C, 0, m * 16, "X", XW, "lu" + C, 0, m, "rg")
        else:
            gather_v("gz" + C, 0, m * 16, "X", XW, "lu" + C, 0, m, "rg")
        vt("fe" + C, 0, m, "cm", j0, j1, "f" + C, 0, m, A.max, "fx")
        vt("fe" + C, m, nl, "sc", b0, b0 + m, "f" + C, m, nl, A.max, "fx")
        vs("ff" + C, 0, nl, "fe" + C, 0, nl, 4095, A.bitwise_and, name="F")
        vs("F16" + C, 0, nl, "ff" + C, 0, nl, -2048.0, A.add, name="F16")
        v(nl, [("FT" + C, 0, nl)], [("F16" + C, 0, nl)], lambda T, g: g.vector.transpose(ap(T, "FT" + C, 0, nl), ap(T, "F16" + C, 0, nl)), "FT", half=True)
        f0, q, l0 = 300 + 16 * c, nl // 16, 16 * t + j0 // 8
        groups(relay("FT" + C, 0, 16, "cm", f0, q), "relayF")
        vs("f0s", l0, l0 + q, "cm", f0, f0 + q, 2048.0, A.add, name="f0s")
        for bb in (0, 1):
            vc("fnat", L * t + 2 * j0 + bb, L * t + 2 * j1, "ff" + C, m * bb, m * bb + m, ost=2, name="fnat")
        v(m * 16, [("rs" + C, 0, m * 16)], [("gz" + C, 0, m * 16), ("smax", 0, m * 16)],
          lambda T, g: g.vector.tensor_tensor_scan(ap(T, "rs" + C, 0, m * 16), ap(T, "smax", 0, m * 16), ap(T, "gz" + C, 0, m * 16), 0.0, A.mult, A.max), "rscan", half=True)
        vc("qs", H * t + j0, H * t + j1, "rs" + C, 15, m * 16, half=True, ist=16, name="qs")

    def send(t, kind, src, s0, s1, dst, d0, d1):
        op("R", 0, [], [(src, s0, s1)], (t, dst, d0, d1, src, s0, s1, "ar_%s%d" % (kind, t)), kind="send", name="send_" + kind)
        op("A", 0, [(dst, d0, d1)], [], "ar_%s%d" % (kind, t), kind="arr", name="arr_" + kind)

    for t in range(TT):
        n = A0 + L * t
        for c, (j0, j1) in enumerate(CH):
            m = j1 - j0
            for b in (0, 1):
                if t:
                    act("pn", L * t + 2 * j0 + b, L * t + 2 * j1, "p", 2 * j0 + b * m, 2 * j0 + b * m + m, F.Copy, ost=2, name="pnat")
        for x in CFG["ORD"].split():
            k, c = x[0], int(x[1]) if len(x) > 1 else 0
            if k == "s":
                send(t, "p", "pn", L * t, L * t + L, "Z", n, n + L)
                if t == 0:
                    setup()
            elif k == "v":
                vstage(t, c, int(x[2]))
            elif k == "p":
                prep(c)
            else:
                {"h": hash_, "z": zstage, "E": elect, "c": choice, "m": common}[k](t, c)
        send(t, "z", "f0s", 16 * t, 16 * t + 12, "f0l", 16 * t, 16 * t + 12)
        send(t, "q", "qs", H * t, H * t + H, "ql", H * t, H * t + H)
        send(t, "f", "fnat", L * t, L * t + L, "R", n, n + L)
        for c, (j0, j1) in enumerate(CH):
            m = j1 - j0
            for b in (0, 1):
                act("pc", 2 * j0 + b * m, 2 * j0 + b * m + m, "Z", n + 2 * j0 + b, n + 2 * j1, F.Identity, ist=2, scale=0.5, bias=1151.25, name="pc")
        vs("Xh", 3712 + H * t, 3712 + H * t + H, "ql", H * t, H * t + H, -0.5, A.mult, half=True, name="Xhrec")
        gather_v("p16", 0, L, "Xh", V, "f0l", 16 * t, 16 * t + 12, "newp", in1=("pc", 0, L), o_=A.add)
        if t < TT - 1:
            vs("p", 0, L, "p16", 0, L, -1024.0, A.add, half=True, name="p")
            vc("X", 3712 + H * t, 3712 + H * t + H, "ql", H * t, H * t + H, half=True, name="Xrec")
            parity()
        else:
            for c, (j0, j1) in enumerate(CH):
                m = j1 - j0
                for b in (0, 1):
                    vs("yo", 2 * j0 + b, 2 * j1, "p16", 2 * j0 + b * m, 2 * j0 + b * m + m, -1024.0, A.add, ost=2, name="yo")
        op("Y", 0, [], [("R", n, n + L)], (lambda T, q, t=t, n=n: q.dma_start(T["yr"][:, L * t:L * t + L], T["R"][:, n:n + L])), kind="store", name="yr")
    op("Y", 0, [], [("yo", 0, L)], (lambda T, q: q.dma_start(T["yp"][:, :], T["yo"][:, :])), kind="store", name="yp")
    return ops


COMP = "VSPG"
ONQ = {"R": "G", "SD": "S"}


def meet(x, y):
    return x[1] < y[2] and y[1] < x[2] and not (x[3] == y[3] and x[4] != y[4])


def deps_of(ops):
    hist, bank = {}, {}
    for i, o in enumerate(ops):
        raw, war = set(), set()
        for x in o["r"]:
            raw |= {j for (y, j, w) in hist.get(x[0], ()) if w and meet(x, y)}
        for x in o["w"]:
            war |= {j for (y, j, w) in hist.get(x[0], ()) if not w and meet(x, y)}
            raw |= {j for (y, j, w) in hist.get(x[0], ()) if w and meet(x, y)}
        for x in o["r"] + o["w"]:
            if x[0] in PS:
                war |= {j for e, j in bank.setdefault(x[0], {}).items() if e != o["e"]}
        for x in o["r"]:
            hist.setdefault(x[0], []).append((x, i, False))
        for x in o["w"]:
            hb = [(y, j, w) for (y, j, w) in hist.get(x[0], ()) if j == i or not (x[1] <= y[1] and y[2] <= x[2] and (x[3] == 1 or x[3:] == y[3:]))]
            hb.append((x, i, True))
            hist[x[0]] = hb
        for x in o["r"] + o["w"]:
            if x[0] in PS:
                bank[x[0]][o["e"]] = i
        raw.discard(i)
        war.discard(i)
        o["raw"], o["war"] = raw, war - raw


def schedule(ops):
    n = len(ops)
    succ = [[] for _ in range(n)]
    wake = EST["wake"]
    for i, o in enumerate(ops):
        al = set(o["raw"]) | set(o["war"])
        if o["k"] == "arr":
            al.add(i - 1)
        o["all"] = al
        for j in al:
            succ[j].append(i)
    cost = [{"send": 300.0, "load": 60.0, "store": 60.0}.get(o["k"], o["c"]) for o in ops]
    lat = [{"load": EST["dma"], "store": EST["dma"], "send": EST["send"]}.get(o["k"], 0.0) + (4000.0 if o["n"] == "ax" else 0.0) for o in ops]
    queue = [ONQ.get(o["e"], o["e"]) for o in ops]
    free_war = lambda i, j: queue[j] == queue[i] and i not in ops[j]["raw"] and ops[i]["k"] == "c"
    prio = [0.0] * n
    for i in range(n - 1, -1, -1):
        prio[i] = max([0.0] + [prio[j] + (0.0 if free_war(i, j) or ops[j]["k"] == "arr" else wake) for j in succ[i]]) + cost[i] + lat[i]
    for i, o in enumerate(ops):
        if o["w"]:
            prio[i] += CFG["PR"].get(o["n"] + o["w"][0][0][-1], 0.0)
    nd = [len(o["all"]) for o in ops]
    ready = [0.0] * n
    free = {q: 0.0 for q in "VSPGYA"}
    avail = {q: [] for q in "VSPGYA"}
    for i in range(n):
        if nd[i] == 0:
            avail[queue[i]].append(i)
    order, busy, start, fin = [], {q: 0.0 for q in "VSPGYA"}, [0.0] * n, [0.0] * n
    while len(order) < n:
        best = None
        for q in avail:
            if avail[q]:
                tmin = min(max(free[q], ready[i]) for i in avail[q])
                i = max((i for i in avail[q] if max(free[q], ready[i]) <= tmin + CFG["SLACK"]), key=lambda i: prio[i])
                st = max(free[q], ready[i])
                if best is None or st < best[0]:
                    best = (st, q, i)
        st, q, i = best
        avail[q].remove(i)
        order.append(i)
        start[i], fin[i] = st, st + cost[i] + lat[i]
        if q != "A":
            free[q] = st + cost[i]
        busy[q] += cost[i]
        for j in succ[i]:
            ready[j] = max(ready[j], st if free_war(i, j) else fin[i] + (0.0 if ops[j]["k"] == "arr" else wake))
            nd[j] -= 1
            if nd[j] == 0:
                avail[queue[j]].append(j)
    return order, max(fin), busy, start, fin


PLAN = []


def plan():
    if PLAN:
        return PLAN[0]
    ops = build()
    deps_of(ops)
    order, end, busy, start, fin = schedule(ops)
    cnt = {e: 0 for e in COMP}
    known = {q: {} for q in "VSPGY"}
    clock, steps, nsent, nst = {}, [], 0, 0
    for i in order:
        o = ops[i]
        e, k = o["e"], o["k"]
        q = ONQ.get(e, e)
        if k == "arr":
            o["sem"] = (o["f"], 16)
            clock[i] = {o["f"]: 16}
            continue
        cl, req = known[q], {}
        for j in o["raw"] | o["war"]:
            p = ops[j]
            pq = ONQ.get(p["e"], p["e"])
            if p["k"] in ("send", "store") or (pq == q and p["k"] == "c" and (j not in o["raw"] or q == "P")):
                continue
            sem, val = p["sem"]
            if cl.get(sem, 0) < val and (sem not in req or ops[req[sem]]["sem"][1] < val):
                req[sem] = j
        for sem in list(req):
            val = ops[req[sem]]["sem"][1]
            if any(s2 != sem and clock[j2].get(sem, 0) >= val for s2, j2 in req.items()):
                del req[sem]
        for sem, j in req.items():
            for a, b in clock[j].items():
                cl[a] = max(cl.get(a, 0), b)
        waits = sorted((sem, ops[j]["sem"][1]) for sem, j in req.items())
        inc = None
        if k == "c":
            cnt[e] += 1
            inc = ("c" + e, 1)
            o["sem"] = ("c" + e, cnt[e])
        elif k == "load":
            inc = o["sem"] = ("ld_" + o["n"], 16)
        elif k == "store":
            nst += 1
            inc = ("stored", 16)
        else:
            nsent += 1
        if "sem" in o:
            clock[i] = dict(cl)
            clock[i][o["sem"][0]] = o["sem"][1]
        steps.append((q, waits, o, inc))
    PLAN.append((steps, cnt, nsent, nst, end, busy, ops, order, start, fin))
    return PLAN[0]


def rank_program(g, core, T, topo):
    rank = T.rank_of(core)
    if rank is None:
        return
    steps, cnt, nsent, nst = plan()[:4]
    qs = {"V": g.vector, "S": g.scalar, "P": g.tensor, "G": g, "Y": g.sync}
    for q, waits, o, inc in steps:
        for sem, val in waits:
            qs[q].wait_ge(T.sem[sem], int(val))
        if o["k"] == "send":
            t, dst, d0, d1, src, s0, s1, ar = o["f"]
            to = T.cores[(rank + 1 + (t % 3)) % len(T.cores)]
            rid, pid, _se = topo.addr(to)
            g.remote_dma(T[dst][:, d0:d1], T[src][:, s0:s1], T.sem[ar], T.sem.sent, pid, rid, topo.mask(core, to))
        elif o["k"] in ("load", "store"):
            o["f"](T, qs[q]).then_inc(T.sem[inc[0]], 16)
        else:
            o["f"](T, g).then_inc(T.sem[inc[0]], 1)
    for e in COMP:
        g.sync.wait_ge(T.sem["c" + e], int(cnt[e]))
    for n in LOADS:
        g.sync.wait_ge(T.sem["ld_" + n], 16)
    for t in range(TT):
        for k in "pfqz":
            g.sync.wait_ge(T.sem["ar_%s%d" % (k, t)], 16)
    g.sync.wait_ge(T.sem.stored, 16 * nst)
    g.wait_ge(T.sem.sent, 16 * nsent)
